import numpy as np
import ml_dtypes


def mxq(x, axis, fmt="e4m3"):
    dtype, down = {"e4m3": (ml_dtypes.float8_e4m3fn, 7), "e5m2": (ml_dtypes.float8_e5m2, 14)}[fmt]
    v = np.moveaxis(np.asarray(x, np.float32).astype(ml_dtypes.bfloat16).astype(np.float64), axis, -1)
    blocks = v.reshape(v.shape[:-1] + (-1, 32))
    amax = np.abs(blocks).max(-1, keepdims=True)
    byte = np.maximum(np.where(amax > 0, np.frexp(amax)[1] - 1 + 127, 0) - down, 1)
    scale = np.exp2(byte - 127.0)
    codes = (blocks / scale).astype(np.float32).astype(dtype).astype(np.float64)
    return np.moveaxis((codes * scale).reshape(v.shape), -1, axis)


WIDE = False


def mx_kscale(k):
    if not WIDE:
        return np.ones(k)
    levels = np.array([10, -10, 5, -5, 0])
    if k % 512:
        return np.exp2(np.random.permutation(np.resize(levels, k // 32))).repeat(32)
    a = np.empty((k // 512, 16))
    for p in range(k // 512):
        a[p, :8] = np.random.permutation(np.resize(levels, 8))
        for g in range(8):
            far = levels[np.abs(levels - a[p, g]) >= 10]
            a[p, g + 8] = far[np.random.randint(len(far))]
    return np.exp2(a.ravel()).repeat(32)


def f64(x):
    return np.asarray(x).astype(np.float64)


def striped(idx):
    return np.tile(idx.reshape(-1, 16).T, (8, 1)).astype(np.uint16)


def unstriped(offs):
    return offs[:16].T.reshape(-1).astype(np.int64)


E2M1 = np.array([0.0, 0.5, 1.0, 1.5, 2.0, 3.0, 4.0, 6.0, -0.0, -0.5, -1.0, -1.5, -2.0, -3.0, -4.0, -6.0])


def pack_weight(w, fmt):
    k, n = w.shape
    w = f64(np.asarray(w, np.float32).astype(ml_dtypes.bfloat16)).reshape(k // 32, 32, n)
    amax = np.abs(w).max(1)
    if fmt == "e4m3":
        byte = np.frexp(amax)[1] - 1 + 127 - 7
    else:
        mant, ex = np.frexp(amax / 6.0)
        byte = np.where(mant > 0.5, ex, ex - 1) + 127
    byte = np.clip(np.where(amax > 0, byte, 1), 1, 254)
    scaled = (w * np.exp2(127.0 - byte)[:, None, :]).reshape(k, n).astype(np.float32)
    by_word = np.ascontiguousarray(scaled.reshape(k // 512, 128, 4, n).transpose(0, 1, 3, 2))
    if fmt == "e4m3":
        words = by_word.astype(ml_dtypes.float8_e4m3fn).view(np.uint8)
    else:
        c = by_word.astype(ml_dtypes.float4_e2m1fn).view(np.uint8) & 0xF
        words = (c[..., 0::2] | (c[..., 1::2] << 4)).reshape(k // 512, 128, 2 * n)
    return np.ascontiguousarray(words), np.ascontiguousarray(byte.astype(np.uint8).reshape(k // 512, 16, n))


def unpack_weight(words, scales, fmt):
    g, _, n = scales.shape
    words = np.ascontiguousarray(words).reshape(g, 128, n, -1)
    if fmt == "e4m3":
        vals = words.view(ml_dtypes.float8_e4m3fn).astype(np.float64)
    else:
        nib = np.empty((g, 128, n, 4), np.uint8)
        nib[..., 0::2] = words & 0xF
        nib[..., 1::2] = words >> 4
        vals = E2M1[nib]
    vals = vals * np.repeat(np.exp2(scales.astype(np.float64) - 127.0), 8, axis=1)[..., None]
    return vals.transpose(0, 1, 3, 2).reshape(g * 512, n)


def gelu(v):
    return 0.5 * v * (1.0 + np.tanh(np.sqrt(2.0 / np.pi) * (v + 0.044715 * v**3)))


K, K2, H, N, T, S, P, T2 = 1024, 512, 1024, 512, 2048, 1024, 512, 2048

def setup_inputs():
    n = np.random.standard_normal
    s = mx_kscale(K)[:, None]
    s2 = mx_kscale(K2)[:, None]
    u = mx_kscale(H)[:, None]
    tab_words, tab_scales = pack_weight(n((K, T)) * s, "e4m3")
    tab2_words, tab2_scales = pack_weight(n((K2, T)) * s2, "e4m3")
    w2_words, w2_scales = pack_weight(n((K2, H)) / np.sqrt(K2) / s2 * u.T, "e2m1")
    w3_words, w3_scales = pack_weight(1.3 * n((H, N)) / np.sqrt(H) / u, "e2m1")
    perm = np.random.permutation(T2)
    return {
        "tab_words": tab_words, "tab_scales": tab_scales,
        "tab2_words": tab2_words, "tab2_scales": tab2_scales,
        "w1": (1.4 * n((K, H)) / np.sqrt(K) / s).astype(np.float32),
        "w2_words": w2_words, "w2_scales": w2_scales,
        "gain": (np.exp(0.3 * n(H)) * u[:, 0]).astype(np.float32),
        "w3_words": w3_words, "w3_scales": w3_scales,
        "w4": (0.8 * n((H, N)) / np.sqrt(H) / u).astype(np.float32),
        "page1": n((N, T2)).astype(np.float32),
        "wg1": np.exp(0.3 * n((128, S))).astype(np.float32),
        "wg2": np.exp(0.3 * n((128, P))).astype(np.float32),
        "offs": striped(np.random.permutation(T)[:S]),
        "offs2": striped(np.random.permutation(T)[:P]),
        "pos1": striped(np.random.permutation(S)[:P]),
        "offs3": striped(perm[:S]),
        "offs4": striped(perm[S:S + P]),
    }

def reference(tab_words, tab_scales, tab2_words, tab2_scales, w1, w2_words, w2_scales, gain, w3_words, w3_scales, w4, page1, wg1, wg2, offs, offs2, pos1, offs3, offs4):
    v = unpack_weight(tab_words, tab_scales, "e4m3")[:, unstriped(offs)]
    v2 = unpack_weight(tab2_words, tab2_scales, "e4m3")[:, unstriped(offs2)]
    h1 = mxq(f64(w1), 0, "e4m3").T @ v
    h2 = unpack_weight(w2_words, w2_scales, "e2m1").T @ v2
    z1 = np.tanh(h1) * f64(gain)[:, None]
    z2 = h2 * h1[:, unstriped(pos1)]
    y1 = unpack_weight(w3_words, w3_scales, "e2m1").T @ mxq(z1, 0, "e4m3")
    y2 = mxq(f64(w4), 0, "e4m3").T @ mxq(z2, 0, "e4m3")
    out = f64(page1).copy()
    out[:, unstriped(offs3)] = np.tile(f64(wg1), (N // 128, 1)) * y1
    out[:, unstriped(offs4)] = np.tile(f64(wg2), (N // 128, 1)) * y2
    return out

@@ -1,0 +1,310 @@
+from contextlib import ExitStack
+
+import concourse.mybir as mybir
+
+K, K2, H, N, T, S, PN, T2 = 1024, 512, 1024, 512, 2048, 1024, 512, 2048
+FLOPS = 2 * (K * H * S + K2 * H * PN + H * N * S + H * N * PN)
+
+F32 = mybir.dt.float32
+BF16 = mybir.dt.bfloat16
+I32 = mybir.dt.int32
+U32 = mybir.dt.uint32
+U16 = mybir.dt.uint16
+U8 = mybir.dt.uint8
+FP8X4 = mybir.dt.float8_e4m3fn_x4
+FP4X4 = mybir.dt.float4_e2m1fn_x4
+MULT = mybir.AluOpType.mult
+TANH = mybir.ActivationFunctionType.Tanh
+COPY = mybir.ActivationFunctionType.Copy
+
+P = 128
+PASS = 512
+NARROW = 256
+
+
+def tile_list_yard_restack_scores_kernel(
+    tc, tab_words, tab_scales, tab2_words, tab2_scales, w1, w2_words, w2_scales, gain,
+    w3_words, w3_scales, w4, page1, wg1, wg2, offs, offs2, pos1, offs3, offs4, out,
+):
+    nc = tc.nc
+    with ExitStack() as ctx:
+        lists = ctx.enter_context(tc.tile_pool(name="lists", bufs=1))
+        keep = ctx.enter_context(tc.tile_pool(name="keep", bufs=1))
+        ring = ctx.enter_context(tc.tile_pool(name="ring", bufs=1))
+        psum = ctx.enter_context(tc.psum_pool(name="psum", bufs=1))
+
+        def held(name, shape, dtype):
+            return keep.tile(shape, dtype, name=name, align_bytes=64)
+
+        def load_list(name, src):
+            tile = lists.tile(list(src.shape), U16, name=name)
+            nc.sync.dma_start(tile[:], src)
+            return tile
+
+        def raw_tile(name):
+            return ring.tile([P, 4, PASS], F32, name=name, tag="raw", bufs=4)
+
+        def rounded_tile(name, width):
+            return ring.tile([P, 4 * width], BF16, name=name, tag="rounded", bufs=4, align_bytes=64)
+
+        def bank(name, tag):
+            return psum.tile([P, PASS], F32, name=name, tag=tag, bufs={"first": 6, "second": 2}[tag])
+
+        def quantize(name, rounded, width):
+            codes = held(name + "_codes", [P, width], U32)
+            plane = held(name + "_plane", [P, width], U8)
+            nc.vector.quantize_mx(out=codes[:].bitcast(FP8X4), scales=plane[:], in_=rounded[:])
+            return codes, plane
+
+        def weave(copy, dst, src):
+            copy(dst[:].rearrange("p (c i j) -> p c j i", i=4, j=4),
+                 src[:].rearrange("p j (c i) -> p c j i", i=4))
+
+        v_words = [held("v_words%d" % a, [P, S], U32) for a in range(2)]
+        v_plane = held("v_plane", [P, S], U8)
+        v2_words = held("v2_words", [P, PN], U32)
+        v2_plane = held("v2_plane", [P, PN], U8)
+        w2_dealt = held("w2_dealt", [P, 2 * H], U8)
+        w2_plane = held("w2_plane", [P, H], U8)
+        w3_sb = held("w3_sb", [P, 2, 2 * N], U8)
+        w3_plane = held("w3_plane", [P, 2, N], U8)
+        gain_sb = held("gain_sb", [P, 2, 4], F32)
+        wg1_sb = held("wg1_sb", [P, S], F32)
+        wg2_sb = held("wg2_sb", [P, PN], F32)
+        pages = [held("page%d" % m, [P, T2], F32) for m in range(4)]
+        h1 = [[held("h1_%d_%d" % (b, t), [P, S], F32) for t in range(4)] for b in range(2)]
+        h2 = [held("h2_%d" % b, [P, 4, PN], F32) for b in range(2)]
+
+        with tc.tile_pool(name="tables", bufs=1) as tables:
+            tab_sb = [tables.tile([P, T], I32, name="tab_sb%d" % a) for a in range(2)]
+            tab2_sb = tables.tile([P, T], I32, name="tab2_sb")
+            tab_bytes = tables.tile([P, T], U8, name="tab_bytes")
+            tab2_bytes = tables.tile([P, T], U8, name="tab2_bytes")
+            w2_sb = tables.tile([P, 2 * H], U8, name="w2_sb")
+            w2_bytes = tables.tile([P, H], U8, name="w2_bytes")
+
+            nc.vector.memset(tab_bytes[:].bitcast(I32), 0)
+            nc.vector.memset(tab2_bytes[:].bitcast(I32), 0)
+            nc.vector.memset(w2_bytes[:].bitcast(I32), 0)
+            nc.vector.memset(w3_plane[:].rearrange("p a n -> p (a n)").bitcast(I32), 0)
+
+            def table_words(words, a):
+                return words[a].rearrange("p t i -> p (t i)").bitcast(I32)
+
+            def load_w1(a, b):
+                raw = raw_tile("w1_raw%d%d" % (a, b))
+                piece = w1[PASS * a : PASS * (a + 1), PASS * b : PASS * (b + 1)]
+                nc.sync.dma_start(raw[:], piece.rearrange("(p j) c -> p j c", j=4))
+                return raw
+
+            def load_scale_rows(plane, rows, scales):
+                for q in range(4):
+                    nc.sync.dma_start(plane[32 * q : 32 * q + rows].bitcast(I32), scales(slice(4 * q, 4 * q + 4)).bitcast(I32))
+
+            def load_page(m):
+                nc.sync.dma_start(pages[m][:], page1[P * m : P * (m + 1), :])
+
+            nc.sync.dma_start(w2_sb[:].bitcast(I32), w2_words[0].bitcast(I32))
+            offs_sb = load_list("offs_sb", offs)
+            load_scale_rows(tab_bytes, 8, lambda r: tab_scales[:, r, :])
+            nc.sync.dma_start(tab_sb[0][:], table_words(tab_words, 0))
+            nc.sync.dma_start(tab2_sb[:], table_words(tab2_words, 0))
+            offs2_sb = load_list("offs2_sb", offs2)
+            load_scale_rows(tab2_bytes, 4, lambda r: tab2_scales[0, r, :])
+            nc.sync.dma_start(tab_sb[1][:], table_words(tab_words, 1))
+            w1_raw = {(0, 0): load_w1(0, 0)}
+            load_scale_rows(w2_bytes, 4, lambda r: w2_scales[0, r, :])
+            for a, b in ((1, 0), (0, 1), (1, 1)):
+                w1_raw[a, b] = load_w1(a, b)
+            nc.sync.dma_start(gain_sb[:], gain.rearrange("(b p t) -> p b t", b=2, t=4))
+            pos_sb = load_list("pos_sb", pos1)
+            nc.sync.dma_start(w3_sb[:].bitcast(I32), w3_words.rearrange("a p c -> p a c").bitcast(I32))
+            nc.sync.dma_start(wg1_sb[:], wg1)
+            load_page(0)
+            load_scale_rows(w3_plane, 4, lambda r: w3_scales[:, r, :].rearrange("a r n -> r a n"))
+            offs3_sb = load_list("offs3_sb", offs3)
+            for m in range(1, 4):
+                load_page(m)
+            offs4_sb = load_list("offs4_sb", offs4)
+            nc.sync.dma_start(wg2_sb[:], wg2)
+
+            for b in range(2):
+                cols = slice(2 * PASS * b, 2 * PASS * (b + 1))
+                nc.vector.tensor_copy(w2_dealt[:, cols].rearrange("p (t q e) -> p q t e", t=4, e=2),
+                                      w2_sb[:, cols].rearrange("p (q t e) -> p q t e", t=4, e=2))
+            nc.vector.tensor_copy(v_plane[:], tab_bytes[:].indirect(offs_sb[:]))
+            nc.vector.tensor_copy(v_words[0][:], tab_sb[0][:].bitcast(U32).indirect(offs_sb[:]))
+            nc.vector.tensor_copy(v2_words[:], tab2_sb[:].bitcast(U32).indirect(offs2_sb[:]))
+            nc.vector.tensor_copy(v2_plane[:], tab2_bytes[:].indirect(offs2_sb[:]))
+            nc.vector.tensor_copy(v_words[1][:], tab_sb[1][:].bitcast(U32).indirect(offs_sb[:]))
+            nc.vector.tensor_copy(w2_plane[:].rearrange("p (b t q) -> p b t q", b=2, t=4),
+                                  w2_bytes[:].rearrange("p (b q t) -> p b t q", b=2, t=4))
+
+        late = ctx.enter_context(tc.tile_pool(name="late", bufs=1))
+
+        w1_q = {}
+        for b in range(2):
+            for a in range(2):
+                rounded = rounded_tile("w1_rounded%d%d" % (a, b), PASS)
+                copy = nc.scalar.copy if (a, b) == (0, 0) else nc.vector.tensor_copy
+                copy(rounded[:].rearrange("p (t m j) -> p m j t", t=4, j=4),
+                     w1_raw[a, b][:].rearrange("p j (m t) -> p m j t", t=4))
+                w1_q[a, b] = quantize("w1_%d%d" % (a, b), rounded, PASS)
+
+        for b in range(2):
+            for t in range(4):
+                col = PASS * b + P * t
+                acc = bank("h2_acc%d%d" % (b, t), "first")
+                nc.tensor.matmul_mx(
+                    out=acc[:], lhsT=w2_dealt[:, 2 * col : 2 * (col + P)].bitcast(FP4X4),
+                    lhsT_scale=w2_plane[:, col : col + P], rhs=v2_words[:].bitcast(FP8X4),
+                    rhs_scale=v2_plane[:], start=True, stop=True)
+                nc.scalar.copy(h2[b][:, t, :], acc[:])
+
+        w4_raw = []
+        for b in range(2):
+            w4_raw.append(raw_tile("w4_raw%d" % b))
+            nc.sync.dma_start(w4_raw[b][:], w4[PASS * b : PASS * (b + 1), :].rearrange("(p j) n -> p j n", j=4))
+
+        def first_stage(acc, b, t, cols):
+            for a in range(2):
+                codes, plane = w1_q[a, b]
+                nc.tensor.matmul_mx(
+                    out=acc, lhsT=codes[:, P * t : P * (t + 1)].bitcast(FP8X4),
+                    lhsT_scale=plane[:, P * t : P * (t + 1)], rhs=v_words[a][:, cols].bitcast(FP8X4),
+                    rhs_scale=v_plane[4 * a :, cols], start=(a == 0), stop=(a == 1))
+
+        def narrow_cols(c):
+            return slice(NARROW * c, NARROW * (c + 1))
+
+        wide_cols = slice(2 * NARROW, S)
+
+        def narrow_sums(b, c):
+            accs = []
+            for u in range(2):
+                acc = bank("h1_acc%d%d%d" % (b, c, u), "first")
+                for e in range(2):
+                    first_stage(acc[:, NARROW * e : NARROW * (e + 1)], b, 2 * u + e, narrow_cols(c))
+                accs.append(acc)
+            return accs
+
+        def narrow_tanh(b, c, accs):
+            th = late.tile([P, 2, NARROW, 2], F32, name="tanh%d%d" % (b, c), tag="tanh_pairs", bufs=3)
+            for u in range(2):
+                nc.scalar.activation(th[:, u, :, :], accs[u][:].rearrange("p (e n) -> p n e", e=2), TANH)
+            return th
+
+        def narrow_keep(b, c, t, accs):
+            u, e = divmod(t, 2)
+            nc.scalar.copy(h1[b][t][:, narrow_cols(c)], accs[u][:, NARROW * e : NARROW * (e + 1)])
+
+        def narrow_z1(b, c, th):
+            rounded = rounded_tile("z1_rounded%d%d" % (b, c), NARROW)
+            factor = gain_sb[:, b, :].rearrange("p (u e) -> p u e", u=2).unsqueeze(1).broadcast_to([P, NARROW, 2, 2])
+            nc.vector.tensor_tensor(rounded[:].rearrange("p (n u e) -> p n u e", u=2, e=2),
+                                    th[:].rearrange("p u n e -> p n u e"), factor, MULT)
+            return quantize("z1_%d%d" % (b, c), rounded, NARROW)
+
+        def score_tile(name):
+            return late.tile([P, PASS], F32, name=name, tag="score", bufs=4)
+
+        def w3_operand(a, m):
+            return w3_sb[:, a, 2 * P * m : 2 * P * (m + 1)].bitcast(FP4X4), w3_plane[:, a, P * m : P * (m + 1)]
+
+        def second_stage(acc, weights, m, z):
+            for a in range(2):
+                lhs, lhs_scale = weights(a, m)
+                nc.tensor.matmul_mx(out=acc, lhsT=lhs, lhsT_scale=lhs_scale, rhs=z[a][0][:].bitcast(FP8X4),
+                                    rhs_scale=z[a][1][:], start=(a == 0), stop=(a == 1))
+
+        def put(m, places, score, factors):
+            nc.vector.tensor_tensor(pages[m][:].indirect(places), score, factors, MULT)
+
+        def narrow_scores(c, u, z):
+            cols = narrow_cols(c)
+            acc = bank("y1_acc%d%d" % (c, u), "second")
+            for e in range(2):
+                second_stage(acc[:, NARROW * e : NARROW * (e + 1)], w3_operand, 2 * u + e, z)
+            score = score_tile("y1_%d%d" % (c, u))
+            nc.scalar.copy(score[:], acc[:])
+            for e in range(2):
+                put(2 * u + e, offs3_sb[:, cols.start // 16 : cols.stop // 16],
+                    score[:, NARROW * e : NARROW * (e + 1)], wg1_sb[:, cols])
+
+        def wide_scores(name, m, weights, z, places, factors, score=None):
+            acc = bank("%s_acc%d" % (name, m), "second")
+            second_stage(acc[:], weights, m, z)
+            if score is None:
+                score = score_tile("%s_%d" % (name, m))
+            nc.scalar.copy(score[:], acc[:])
+            put(m, places, score[:], factors)
+
+        def wide_keep(b, t):
+            acc = bank("h1_wide%d%d" % (b, t), "first")
+            first_stage(acc[:], b, t, wide_cols)
+            nc.scalar.copy(h1[b][t][:, wide_cols], acc[:])
+
+        def lead_product(prod, b, t):
+            nc.vector.tensor_tensor(prod[:, t, :], h1[b][t][:].indirect(pos_sb[:]), h2[b][:, t, :], MULT)
+
+        def wide_planes(b):
+            planes = late.tile([P, 4, PASS], BF16, name="z1_planes%d" % b, tag="z1_planes", bufs=1)
+            for t in range(4):
+                th = late.tile([P, PASS], F32, name="tanh_wide%d%d" % (b, t), tag="tanh_wide", bufs=3)
+                nc.scalar.activation(th[:], h1[b][t][:, wide_cols], TANH)
+                nc.scalar.activation(planes[:, t, :], th[:], COPY, scale=gain_sb[:, b, t : t + 1])
+            return planes
+
+        def weave_quantize(name, src):
+            rounded = rounded_tile(name + "_rounded", PASS)
+            weave(nc.scalar.copy, rounded, src)
+            return quantize(name, rounded, PASS)
+
+        def w4_operand(a, m):
+            codes, plane = w4_q[a]
+            return codes[:, P * m : P * (m + 1)].bitcast(FP8X4), plane[:, P * m : P * (m + 1)]
+
+        z1_first = []
+        for b in range(2):
+            accs = narrow_sums(b, 0)
+            z1_first.append(narrow_z1(b, 0, narrow_tanh(b, 0, accs)))
+            for t in range(4):
+                narrow_keep(b, 0, t, accs)
+        for u in range(2):
+            narrow_scores(0, u, z1_first)
+
+        z1_second = []
+        prods = []
+        for b in range(2):
+            accs = narrow_sums(b, 1)
+            prods.append(raw_tile("z2_raw%d" % b))
+            if b == 1:
+                th = narrow_tanh(b, 1, accs)
+                z1_second.append(narrow_z1(b, 1, th))
+            for t in range(4):
+                narrow_keep(b, 1, t, accs)
+                wide_keep(b, t)
+                lead_product(prods[b], b, t)
+            if b == 0:
+                th = narrow_tanh(b, 1, accs)
+                z1_second.append(narrow_z1(b, 1, th))
+
+        w4_q = [weave_quantize("w4_%d" % b, w4_raw[b]) for b in range(2)]
+        narrow_scores(1, 0, z1_second)
+        z2 = [weave_quantize("z2_%d" % b, prods[b]) for b in range(2)]
+        narrow_scores(1, 1, z1_second)
+
+        def call_scores(m, score=None):
+            wide_scores("y2", m, w4_operand, z2, offs4_sb[:], wg2_sb[:], score)
+
+        planes = wide_planes(0)
+        call_scores(0)
+        call_scores(1)
+        z1_third = [weave_quantize("z1_02", planes)]
+        call_scores(2)
+        z1_third.append(weave_quantize("z1_12", wide_planes(1)))
+        call_scores(3, late.tile([P, PASS], F32, name="y2_last", tag="z1_planes", bufs=1))
+        for m in range(4):
+            wide_scores("y1_wide", m, w3_operand, z1_third,
+                        offs3_sb[:, wide_cols.start // 16 : wide_cols.stop // 16], wg1_sb[:, wide_cols])
+            nc.sync.dma_start(out[P * m : P * (m + 1), :], pages[m][:])

@@ -19,7 +19,9 @@ COPY = mybir.ActivationFunctionType.Copy
 
 P = 128
 PASS = 512
-NARROW = 256
+BANK = 512
+HEAD = 256
+REST = S - HEAD
 
 
 def tile_list_yard_restack_scores_kernel(
@@ -44,27 +46,46 @@ def tile_list_yard_restack_scores_kernel(
         def raw_tile(name):
             return ring.tile([P, 4, PASS], F32, name=name, tag="raw", bufs=4)
 
-        def rounded_tile(name, width):
-            return ring.tile([P, 4 * width], BF16, name=name, tag="rounded", bufs=4, align_bytes=64)
+        def rounded_tile(name, width, tag="rounded", bufs=4):
+            return ring.tile([P, 4 * width], BF16, name=name, tag=tag, bufs=bufs, align_bytes=64)
 
         def bank(name, tag):
-            return psum.tile([P, PASS], F32, name=name, tag=tag, bufs={"first": 6, "second": 2}[tag])
+            return psum.tile([P, BANK], F32, name=name, tag=tag, bufs={"first": 6, "second": 2}[tag])
 
         def quantize(name, rounded, width):
             codes = held(name + "_codes", [P, width], U32)
             plane = held(name + "_plane", [P, width], U8)
-            nc.vector.quantize_mx(out=codes[:].bitcast(FP8X4), scales=plane[:], in_=rounded[:])
+            for lo in range(0, width, BANK):
+                hi = min(lo + BANK, width)
+                nc.vector.quantize_mx(out=codes[:, lo:hi].bitcast(FP8X4), scales=plane[:, lo:hi],
+                                      in_=rounded[:, 4 * lo : 4 * hi])
             return codes, plane
 
-        def weave(copy, dst, src):
-            copy(dst[:].rearrange("p (c i j) -> p c j i", i=4, j=4),
-                 src[:].rearrange("p j (c i) -> p c j i", i=4))
+        def weave_quantize(name, src, width, tag="rounded", bufs=4):
+            rounded = rounded_tile(name + "_rounded", width, tag, bufs)
+            nc.scalar.copy(rounded[:].rearrange("p (c i j) -> p c j i", i=4, j=4),
+                           src[:].rearrange("p j (c i) -> p c j i", i=4))
+            return quantize(name, rounded, width)
+
+        def table_words(words, a):
+            return words[a].rearrange("p t i -> p (t i)").bitcast(I32)
+
+        def load_scale_rows(plane, first, rows, scales):
+            for q in range(4):
+                lo = 32 * q + first
+                nc.sync.dma_start(plane[lo : lo + rows].bitcast(I32), scales(slice(4 * q, 4 * q + 4)).bitcast(I32))
+
+        def load_page(m):
+            nc.sync.dma_start(pages[m][:], page1[P * m : P * (m + 1), :])
 
         v_words = [held("v_words%d" % a, [P, S], U32) for a in range(2)]
         v_plane = held("v_plane", [P, S], U8)
+        tab2_sb = held("tab2_sb", [P, T], I32)
+        tab2_bytes = held("tab2_bytes", [P, T], U8)
         v2_words = held("v2_words", [P, PN], U32)
         v2_plane = held("v2_plane", [P, PN], U8)
         w2_dealt = held("w2_dealt", [P, 2 * H], U8)
+        w2_bytes = held("w2_bytes", [P, H], U8)
         w2_plane = held("w2_plane", [P, H], U8)
         w3_sb = held("w3_sb", [P, 2, 2 * N], U8)
         w3_plane = held("w3_plane", [P, 2, N], U8)
@@ -72,59 +93,46 @@ def tile_list_yard_restack_scores_kernel(
         wg1_sb = held("wg1_sb", [P, S], F32)
         wg2_sb = held("wg2_sb", [P, PN], F32)
         pages = [held("page%d" % m, [P, T2], F32) for m in range(4)]
-        h1 = [[held("h1_%d_%d" % (b, t), [P, S], F32) for t in range(4)] for b in range(2)]
-        h2 = [held("h2_%d" % b, [P, 4, PN], F32) for b in range(2)]
+        h1 = [held("h1_%d" % b, [P, 4, S], F32) for b in range(2)]
 
         with tc.tile_pool(name="tables", bufs=1) as tables:
             tab_sb = [tables.tile([P, T], I32, name="tab_sb%d" % a) for a in range(2)]
-            tab2_sb = tables.tile([P, T], I32, name="tab2_sb")
             tab_bytes = tables.tile([P, T], U8, name="tab_bytes")
-            tab2_bytes = tables.tile([P, T], U8, name="tab2_bytes")
             w2_sb = tables.tile([P, 2 * H], U8, name="w2_sb")
-            w2_bytes = tables.tile([P, H], U8, name="w2_bytes")
 
             nc.vector.memset(tab_bytes[:].bitcast(I32), 0)
+            nc.vector.memset(w3_plane[:].rearrange("p a n -> p (a n)").bitcast(I32), 0)
             nc.vector.memset(tab2_bytes[:].bitcast(I32), 0)
             nc.vector.memset(w2_bytes[:].bitcast(I32), 0)
-            nc.vector.memset(w3_plane[:].rearrange("p a n -> p (a n)").bitcast(I32), 0)
-
-            def table_words(words, a):
-                return words[a].rearrange("p t i -> p (t i)").bitcast(I32)
-
-            def load_w1(a, b):
-                raw = raw_tile("w1_raw%d%d" % (a, b))
-                piece = w1[PASS * a : PASS * (a + 1), PASS * b : PASS * (b + 1)]
-                nc.sync.dma_start(raw[:], piece.rearrange("(p j) c -> p j c", j=4))
-                return raw
-
-            def load_scale_rows(plane, rows, scales):
-                for q in range(4):
-                    nc.sync.dma_start(plane[32 * q : 32 * q + rows].bitcast(I32), scales(slice(4 * q, 4 * q + 4)).bitcast(I32))
-
-            def load_page(m):
-                nc.sync.dma_start(pages[m][:], page1[P * m : P * (m + 1), :])
 
             nc.sync.dma_start(w2_sb[:].bitcast(I32), w2_words[0].bitcast(I32))
             offs_sb = load_list("offs_sb", offs)
-            load_scale_rows(tab_bytes, 8, lambda r: tab_scales[:, r, :])
             nc.sync.dma_start(tab_sb[0][:], table_words(tab_words, 0))
-            nc.sync.dma_start(tab2_sb[:], table_words(tab2_words, 0))
-            offs2_sb = load_list("offs2_sb", offs2)
-            load_scale_rows(tab2_bytes, 4, lambda r: tab2_scales[0, r, :])
+            load_scale_rows(tab_bytes, 4, 8, lambda r: tab_scales[:, r, :])
             nc.sync.dma_start(tab_sb[1][:], table_words(tab_words, 1))
-            w1_raw = {(0, 0): load_w1(0, 0)}
-            load_scale_rows(w2_bytes, 4, lambda r: w2_scales[0, r, :])
-            for a, b in ((1, 0), (0, 1), (1, 1)):
-                w1_raw[a, b] = load_w1(a, b)
+            w1_raw = {}
+            for b in range(2):
+                for a in range(2):
+                    w1_raw[a, b] = raw_tile("w1_raw%d%d" % (a, b))
+                    piece = w1[PASS * a : PASS * (a + 1), PASS * b : PASS * (b + 1)]
+                    nc.sync.dma_start(w1_raw[a, b][:], piece.rearrange("(p j) c -> p j c", j=4))
             nc.sync.dma_start(gain_sb[:], gain.rearrange("(b p t) -> p b t", b=2, t=4))
             pos_sb = load_list("pos_sb", pos1)
             nc.sync.dma_start(w3_sb[:].bitcast(I32), w3_words.rearrange("a p c -> p a c").bitcast(I32))
             nc.sync.dma_start(wg1_sb[:], wg1)
             load_page(0)
-            load_scale_rows(w3_plane, 4, lambda r: w3_scales[:, r, :].rearrange("a r n -> r a n"))
+            load_scale_rows(w3_plane, 0, 4, lambda r: w3_scales[:, r, :].rearrange("a r n -> r a n"))
             offs3_sb = load_list("offs3_sb", offs3)
-            for m in range(1, 4):
-                load_page(m)
+            load_page(1)
+            load_scale_rows(w2_bytes, 0, 4, lambda r: w2_scales[0, r, :])
+            offs2_sb = load_list("offs2_sb", offs2)
+            nc.sync.dma_start(tab2_sb[:], table_words(tab2_words, 0))
+            load_scale_rows(tab2_bytes, 0, 4, lambda r: tab2_scales[0, r, :])
+            w4_raw = [raw_tile("w4_raw%d" % b) for b in range(2)]
+            nc.sync.dma_start(w4_raw[0][:], w4[0:PASS, :].rearrange("(p j) n -> p j n", j=4))
+            nc.sync.dma_start(w4_raw[1][:], w4[PASS:H, :].rearrange("(p j) n -> p j n", j=4))
+            load_page(2)
+            load_page(3)
             offs4_sb = load_list("offs4_sb", offs4)
             nc.sync.dma_start(wg2_sb[:], wg2)
 
@@ -132,13 +140,9 @@ def tile_list_yard_restack_scores_kernel(
                 cols = slice(2 * PASS * b, 2 * PASS * (b + 1))
                 nc.vector.tensor_copy(w2_dealt[:, cols].rearrange("p (t q e) -> p q t e", t=4, e=2),
                                       w2_sb[:, cols].rearrange("p (q t e) -> p q t e", t=4, e=2))
-            nc.vector.tensor_copy(v_plane[:], tab_bytes[:].indirect(offs_sb[:]))
             nc.vector.tensor_copy(v_words[0][:], tab_sb[0][:].bitcast(U32).indirect(offs_sb[:]))
-            nc.vector.tensor_copy(v2_words[:], tab2_sb[:].bitcast(U32).indirect(offs2_sb[:]))
-            nc.vector.tensor_copy(v2_plane[:], tab2_bytes[:].indirect(offs2_sb[:]))
+            nc.vector.tensor_copy(v_plane[:], tab_bytes[:].indirect(offs_sb[:]))
             nc.vector.tensor_copy(v_words[1][:], tab_sb[1][:].bitcast(U32).indirect(offs_sb[:]))
-            nc.vector.tensor_copy(w2_plane[:].rearrange("p (b t q) -> p b t q", b=2, t=4),
-                                  w2_bytes[:].rearrange("p (b q t) -> p b t q", b=2, t=4))
 
         late = ctx.enter_context(tc.tile_pool(name="late", bufs=1))
 
@@ -151,160 +155,136 @@ def tile_list_yard_restack_scores_kernel(
                      w1_raw[a, b][:].rearrange("p j (m t) -> p m j t", t=4))
                 w1_q[a, b] = quantize("w1_%d%d" % (a, b), rounded, PASS)
 
-        for b in range(2):
-            for t in range(4):
-                col = PASS * b + P * t
-                acc = bank("h2_acc%d%d" % (b, t), "first")
-                nc.tensor.matmul_mx(
-                    out=acc[:], lhsT=w2_dealt[:, 2 * col : 2 * (col + P)].bitcast(FP4X4),
-                    lhsT_scale=w2_plane[:, col : col + P], rhs=v2_words[:].bitcast(FP8X4),
-                    rhs_scale=v2_plane[:], start=True, stop=True)
-                nc.scalar.copy(h2[b][:, t, :], acc[:])
-
-        w4_raw = []
-        for b in range(2):
-            w4_raw.append(raw_tile("w4_raw%d" % b))
-            nc.sync.dma_start(w4_raw[b][:], w4[PASS * b : PASS * (b + 1), :].rearrange("(p j) n -> p j n", j=4))
-
         def first_stage(acc, b, t, cols):
             for a in range(2):
                 codes, plane = w1_q[a, b]
                 nc.tensor.matmul_mx(
                     out=acc, lhsT=codes[:, P * t : P * (t + 1)].bitcast(FP8X4),
                     lhsT_scale=plane[:, P * t : P * (t + 1)], rhs=v_words[a][:, cols].bitcast(FP8X4),
-                    rhs_scale=v_plane[4 * a :, cols], start=(a == 0), stop=(a == 1))
+                    rhs_scale=v_plane[4 * a + 4 :, cols], start=(a == 0), stop=(a == 1))
 
-        def narrow_cols(c):
-            return slice(NARROW * c, NARROW * (c + 1))
+        def pair_sums(b, u, cols):
+            acc = bank("h1_pair%d%d_%d" % (b, u, cols.start), "first")
+            for e in range(2):
+                first_stage(acc[:, HEAD * e : HEAD * (e + 1)], b, 2 * u + e, cols)
+            return acc
 
-        wide_cols = slice(2 * NARROW, S)
-
-        def narrow_sums(b, c):
-            accs = []
-            for u in range(2):
-                acc = bank("h1_acc%d%d%d" % (b, c, u), "first")
-                for e in range(2):
-                    first_stage(acc[:, NARROW * e : NARROW * (e + 1)], b, 2 * u + e, narrow_cols(c))
-                accs.append(acc)
-            return accs
-
-        def narrow_tanh(b, c, accs):
-            th = late.tile([P, 2, NARROW, 2], F32, name="tanh%d%d" % (b, c), tag="tanh_pairs", bufs=3)
-            for u in range(2):
-                nc.scalar.activation(th[:, u, :, :], accs[u][:].rearrange("p (e n) -> p n e", e=2), TANH)
-            return th
-
-        def narrow_keep(b, c, t, accs):
-            u, e = divmod(t, 2)
-            nc.scalar.copy(h1[b][t][:, narrow_cols(c)], accs[u][:, NARROW * e : NARROW * (e + 1)])
-
-        def narrow_z1(b, c, th):
-            rounded = rounded_tile("z1_rounded%d%d" % (b, c), NARROW)
-            factor = gain_sb[:, b, :].rearrange("p (u e) -> p u e", u=2).unsqueeze(1).broadcast_to([P, NARROW, 2, 2])
-            nc.vector.tensor_tensor(rounded[:].rearrange("p (n u e) -> p n u e", u=2, e=2),
-                                    th[:].rearrange("p u n e -> p n u e"), factor, MULT)
-            return quantize("z1_%d%d" % (b, c), rounded, NARROW)
-
-        def score_tile(name):
-            return late.tile([P, PASS], F32, name=name, tag="score", bufs=4)
+        def pair_keep(b, u, cols, acc):
+            nc.scalar.copy(h1[b][:, 2 * u : 2 * u + 2, cols], acc[:].rearrange("p (e n) -> p e n", e=2))
 
         def w3_operand(a, m):
             return w3_sb[:, a, 2 * P * m : 2 * P * (m + 1)].bitcast(FP4X4), w3_plane[:, a, P * m : P * (m + 1)]
-
-        def second_stage(acc, weights, m, z):
-            for a in range(2):
-                lhs, lhs_scale = weights(a, m)
-                nc.tensor.matmul_mx(out=acc, lhsT=lhs, lhsT_scale=lhs_scale, rhs=z[a][0][:].bitcast(FP8X4),
-                                    rhs_scale=z[a][1][:], start=(a == 0), stop=(a == 1))
-
-        def put(m, places, score, factors):
-            nc.vector.tensor_tensor(pages[m][:].indirect(places), score, factors, MULT)
-
-        def narrow_scores(c, u, z):
-            cols = narrow_cols(c)
-            acc = bank("y1_acc%d%d" % (c, u), "second")
-            for e in range(2):
-                second_stage(acc[:, NARROW * e : NARROW * (e + 1)], w3_operand, 2 * u + e, z)
-            score = score_tile("y1_%d%d" % (c, u))
-            nc.scalar.copy(score[:], acc[:])
-            for e in range(2):
-                put(2 * u + e, offs3_sb[:, cols.start // 16 : cols.stop // 16],
-                    score[:, NARROW * e : NARROW * (e + 1)], wg1_sb[:, cols])
-
-        def wide_scores(name, m, weights, z, places, factors, score=None):
-            acc = bank("%s_acc%d" % (name, m), "second")
-            second_stage(acc[:], weights, m, z)
-            if score is None:
-                score = score_tile("%s_%d" % (name, m))
-            nc.scalar.copy(score[:], acc[:])
-            put(m, places, score[:], factors)
-
-        def wide_keep(b, t):
-            acc = bank("h1_wide%d%d" % (b, t), "first")
-            first_stage(acc[:], b, t, wide_cols)
-            nc.scalar.copy(h1[b][t][:, wide_cols], acc[:])
-
-        def lead_product(prod, b, t):
-            nc.vector.tensor_tensor(prod[:, t, :], h1[b][t][:].indirect(pos_sb[:]), h2[b][:, t, :], MULT)
-
-        def wide_planes(b):
-            planes = late.tile([P, 4, PASS], BF16, name="z1_planes%d" % b, tag="z1_planes", bufs=1)
-            for t in range(4):
-                th = late.tile([P, PASS], F32, name="tanh_wide%d%d" % (b, t), tag="tanh_wide", bufs=3)
-                nc.scalar.activation(th[:], h1[b][t][:, wide_cols], TANH)
-                nc.scalar.activation(planes[:, t, :], th[:], COPY, scale=gain_sb[:, b, t : t + 1])
-            return planes
-
-        def weave_quantize(name, src):
-            rounded = rounded_tile(name + "_rounded", PASS)
-            weave(nc.scalar.copy, rounded, src)
-            return quantize(name, rounded, PASS)
 
         def w4_operand(a, m):
             codes, plane = w4_q[a]
             return codes[:, P * m : P * (m + 1)].bitcast(FP8X4), plane[:, P * m : P * (m + 1)]
 
-        z1_first = []
+        def second_stage(acc, weights, m, z, cols):
+            for a in range(2):
+                lhs, lhs_scale = weights(a, m)
+                nc.tensor.matmul_mx(out=acc, lhsT=lhs, lhsT_scale=lhs_scale, rhs=z[a][0][:, cols].bitcast(FP8X4),
+                                    rhs_scale=z[a][1][:, cols], start=(a == 0), stop=(a == 1))
+
+        def score_tile(name, width):
+            return late.tile([P, width], F32, name=name, tag="score", bufs=4)
+
+        def put(m, places, score, factors):
+            nc.vector.tensor_tensor(pages[m][:].indirect(places), score, factors, MULT)
+
+        head_cols = slice(0, HEAD)
+        z1_head = []
         for b in range(2):
-            accs = narrow_sums(b, 0)
-            z1_first.append(narrow_z1(b, 0, narrow_tanh(b, 0, accs)))
-            for t in range(4):
-                narrow_keep(b, 0, t, accs)
-        for u in range(2):
-            narrow_scores(0, u, z1_first)
+            accs = [pair_sums(b, u, head_cols) for u in range(2)]
+            th = late.tile([P, 2, HEAD, 2], F32, name="tanh_head%d" % b, tag="tanh_head", bufs=2)
+            for u in range(2):
+                nc.scalar.activation(th[:, u, :, :], accs[u][:].rearrange("p (e n) -> p n e", e=2), TANH)
+            rounded = rounded_tile("z1_head_rounded%d" % b, HEAD)
+            factor = gain_sb[:, b, :].rearrange("p (u e) -> p u e", u=2).unsqueeze(1).broadcast_to([P, HEAD, 2, 2])
+            nc.vector.tensor_tensor(rounded[:].rearrange("p (n u e) -> p n u e", u=2, e=2),
+                                    th[:].rearrange("p u n e -> p n u e"), factor, MULT)
+            z1_head.append(quantize("z1_head%d" % b, rounded, HEAD))
+            for u in range(2):
+                pair_keep(b, u, head_cols, accs[u])
 
-        z1_second = []
-        prods = []
+        def head_scores(u, score):
+            acc = bank("y1_head_acc%d" % u, "second")
+            for e in range(2):
+                second_stage(acc[:, HEAD * e : HEAD * (e + 1)], w3_operand, 2 * u + e, z1_head, head_cols)
+            nc.scalar.copy(score[:], acc[:])
+            for e in range(2):
+                put(2 * u + e, offs3_sb[:, : HEAD // 16], score[:, HEAD * e : HEAD * (e + 1)], wg1_sb[:, head_cols])
+
+        head_scores(0, score_tile("y1_head0", BANK))
+
+        leads = []
         for b in range(2):
-            accs = narrow_sums(b, 1)
-            prods.append(raw_tile("z2_raw%d" % b))
-            if b == 1:
-                th = narrow_tanh(b, 1, accs)
-                z1_second.append(narrow_z1(b, 1, th))
-            for t in range(4):
-                narrow_keep(b, 1, t, accs)
-                wide_keep(b, t)
-                lead_product(prods[b], b, t)
-            if b == 0:
-                th = narrow_tanh(b, 1, accs)
-                z1_second.append(narrow_z1(b, 1, th))
+            leads.append(raw_tile("lead%d" % b))
+            for u in range(2):
+                cols = slice(HEAD, 2 * HEAD)
+                pair_keep(b, u, cols, pair_sums(b, u, cols))
+                for t in (2 * u, 2 * u + 1):
+                    acc = bank("h1_wide%d%d" % (b, t), "first")
+                    first_stage(acc[:], b, t, slice(2 * HEAD, S))
+                    nc.scalar.copy(h1[b][:, t, 2 * HEAD :], acc[:])
+                    nc.vector.tensor_copy(leads[b][:, t, :], h1[b][:, t, :].indirect(pos_sb[:]))
 
-        w4_q = [weave_quantize("w4_%d" % b, w4_raw[b]) for b in range(2)]
-        narrow_scores(1, 0, z1_second)
-        z2 = [weave_quantize("z2_%d" % b, prods[b]) for b in range(2)]
-        narrow_scores(1, 1, z1_second)
+        nc.vector.tensor_copy(v2_words[:], tab2_sb[:].bitcast(U32).indirect(offs2_sb[:]))
+        nc.vector.tensor_copy(v2_plane[:], tab2_bytes[:].indirect(offs2_sb[:]))
+        nc.vector.tensor_copy(w2_plane[:].rearrange("p (b t q) -> p b t q", b=2, t=4),
+                              w2_bytes[:].rearrange("p (b q t) -> p b t q", b=2, t=4))
 
-        def call_scores(m, score=None):
-            wide_scores("y2", m, w4_operand, z2, offs4_sb[:], wg2_sb[:], score)
+        z2 = []
+        for b in range(2):
+            rounded = rounded_tile("z2_rounded%d" % b, PN, "z2_rounded%d" % b, 1)
+            for c in range(PN // P):
+                cols = slice(P * c, P * (c + 1))
+                acc = bank("h2_acc%d%d" % (b, c), "first")
+                for t in range(4):
+                    col = PASS * b + P * t
+                    nc.tensor.matmul_mx(
+                        out=acc[:, P * t : P * (t + 1)], lhsT=w2_dealt[:, 2 * col : 2 * (col + P)].bitcast(FP4X4),
+                        lhsT_scale=w2_plane[:, col : col + P], rhs=v2_words[:, cols].bitcast(FP8X4),
+                        rhs_scale=v2_plane[:, cols], start=True, stop=True)
+                nc.vector.tensor_tensor(
+                    rounded[:, 4 * P * c : 4 * P * (c + 1)].rearrange("p (n i t) -> p n t i", i=2, t=4),
+                    acc[:].rearrange("p (t n i) -> p n t i", t=4, i=2),
+                    leads[b][:, :, cols].rearrange("p t (n i) -> p n t i", i=2), MULT)
+            z2.append(quantize("z2_%d" % b, rounded, PN))
 
-        planes = wide_planes(0)
-        call_scores(0)
-        call_scores(1)
-        z1_third = [weave_quantize("z1_02", planes)]
-        call_scores(2)
-        z1_third.append(weave_quantize("z1_12", wide_planes(1)))
-        call_scores(3, late.tile([P, PASS], F32, name="y2_last", tag="z1_planes", bufs=1))
+        def planes_tile(b):
+            return late.tile([P, 4, REST], BF16, name="z1_planes%d" % b, tag="z1_planes", bufs=1)
+
+        def rest_plane(planes, b, t):
+            th = late.tile([P, REST], F32, name="tanh_rest%d%d" % (b, t), tag="tanh_rest", bufs=3)
+            nc.scalar.activation(th[:], h1[b][:, t, HEAD:], TANH)
+            nc.scalar.activation(planes[:, t, :], th[:], COPY, scale=gain_sb[:, b, t : t + 1])
+
+        def call_scores(m, score):
+            acc = bank("y2_acc%d" % m, "first")
+            second_stage(acc[:], w4_operand, m, z2, slice(0, PN))
+            nc.scalar.copy(score[:], acc[:])
+            put(m, offs4_sb[:], score[:], wg2_sb[:])
+
+        planes = planes_tile(0)
+        for t in range(4):
+            rest_plane(planes, 0, t)
+        w4_q = [weave_quantize("w4_%d" % b, w4_raw[b], N) for b in range(2)]
+        z1_rest = [weave_quantize("z1_rest0", planes, REST, "rest_rounded", 1)]
+        head_scores(1, ring.tile([P, BANK], F32, name="y1_head1", tag="z2_rounded1", bufs=1, align_bytes=64))
+        planes = planes_tile(1)
+        for t in range(4):
+            rest_plane(planes, 1, t)
+            if t > 0:
+                call_scores(t - 1, score_tile("y2_%d" % (t - 1), PN))
+        z1_rest.append(weave_quantize("z1_rest1", planes, REST, "rest_rounded", 1))
+        call_scores(3, late.tile([P, PN], F32, name="y2_last", tag="z1_planes", bufs=1))
+
         for m in range(4):
-            wide_scores("y1_wide", m, w3_operand, z1_third,
-                        offs3_sb[:, wide_cols.start // 16 : wide_cols.stop // 16], wg1_sb[:, wide_cols])
+            score = score_tile("y1_rest%d" % m, REST)
+            for lo in range(0, REST, BANK):
+                cols = slice(lo, min(lo + BANK, REST))
+                acc = bank("y1_rest_acc%d_%d" % (m, lo), "first")
+                second_stage(acc[:, : cols.stop - lo], w3_operand, m, z1_rest, cols)
+                nc.scalar.copy(score[:, cols], acc[:, : cols.stop - lo])
+            put(m, offs3_sb[:, HEAD // 16 :], score[:], wg1_sb[:, HEAD:])
             nc.sync.dma_start(out[P * m : P * (m + 1), :], pages[m][:])

@@ -19,9 +19,7 @@ COPY = mybir.ActivationFunctionType.Copy
 
 P = 128
 PASS = 512
-BANK = 512
-HEAD = 256
-REST = S - HEAD
+W = 512
 
 
 def tile_list_yard_restack_scores_kernel(
@@ -43,29 +41,31 @@ def tile_list_yard_restack_scores_kernel(
             nc.sync.dma_start(tile[:], src)
             return tile
 
-        def raw_tile(name):
-            return ring.tile([P, 4, PASS], F32, name=name, tag="raw", bufs=4)
+        def raw_tile(name, room):
+            return ring.tile([P, 4, W], F32, name=name, tag="raw%d" % room, align_bytes=64)
 
-        def rounded_tile(name, width, tag="rounded", bufs=4):
-            return ring.tile([P, 4 * width], BF16, name=name, tag=tag, bufs=bufs, align_bytes=64)
+        def rounded_tile(name, room):
+            return ring.tile([P, 2 * 4 * W], BF16, name=name, tag="rounded%d" % room, align_bytes=64)
 
-        def bank(name, tag):
-            return psum.tile([P, BANK], F32, name=name, tag=tag, bufs={"first": 6, "second": 2}[tag])
+        def half(rounded, a):
+            return rounded[:, 4 * W * a : 4 * W * (a + 1)]
 
-        def quantize(name, rounded, width):
-            codes = held(name + "_codes", [P, width], U32)
-            plane = held(name + "_plane", [P, width], U8)
-            for lo in range(0, width, BANK):
-                hi = min(lo + BANK, width)
-                nc.vector.quantize_mx(out=codes[:, lo:hi].bitcast(FP8X4), scales=plane[:, lo:hi],
-                                      in_=rounded[:, 4 * lo : 4 * hi])
-            return codes, plane
+        banks = []
 
-        def weave_quantize(name, src, width, tag="rounded", bufs=4):
-            rounded = rounded_tile(name + "_rounded", width, tag, bufs)
-            nc.scalar.copy(rounded[:].rearrange("p (c i j) -> p c j i", i=4, j=4),
+        def bank(name):
+            banks.append(psum.tile([P, W], F32, name=name, tag="bank%d" % (len(banks) % 8), bufs=1))
+            return banks[-1]
+
+        def operand_tiles(name):
+            return held(name + "_codes", [P, 2 * W], U32), held(name + "_plane", [P, 2 * W], U8)
+
+        def quantize(operand, first, rounded):
+            cols = slice(first, first + rounded.shape[1] // 4)
+            nc.vector.quantize_mx(out=operand[0][:, cols].bitcast(FP8X4), scales=operand[1][:, cols], in_=rounded)
+
+        def weave(dst, src):
+            nc.scalar.copy(dst.rearrange("p (c i j) -> p c j i", i=4, j=4),
                            src[:].rearrange("p j (c i) -> p c j i", i=4))
-            return quantize(name, rounded, width)
 
         def table_words(words, a):
             return words[a].rearrange("p t i -> p (t i)").bitcast(I32)
@@ -75,17 +75,22 @@ def tile_list_yard_restack_scores_kernel(
                 lo = 32 * q + first
                 nc.sync.dma_start(plane[lo : lo + rows].bitcast(I32), scales(slice(4 * q, 4 * q + 4)).bitcast(I32))
 
+        def load_rows(name, room, rows):
+            raw = raw_tile(name, room)
+            nc.sync.dma_start(raw[:], rows.rearrange("(p j) c -> p j c", j=4))
+            return raw
+
+        def load_w1(a, b):
+            return load_rows("w1_raw%d%d" % (a, b), 2 * b + a, w1[PASS * a : PASS * (a + 1), W * b : W * (b + 1)])
+
         def load_page(m):
             nc.sync.dma_start(pages[m][:], page1[P * m : P * (m + 1), :])
 
         v_words = [held("v_words%d" % a, [P, S], U32) for a in range(2)]
         v_plane = held("v_plane", [P, S], U8)
-        tab2_sb = held("tab2_sb", [P, T], I32)
-        tab2_bytes = held("tab2_bytes", [P, T], U8)
         v2_words = held("v2_words", [P, PN], U32)
         v2_plane = held("v2_plane", [P, PN], U8)
         w2_dealt = held("w2_dealt", [P, 2 * H], U8)
-        w2_bytes = held("w2_bytes", [P, H], U8)
         w2_plane = held("w2_plane", [P, H], U8)
         w3_sb = held("w3_sb", [P, 2, 2 * N], U8)
         w3_plane = held("w3_plane", [P, 2, N], U8)
@@ -93,198 +98,173 @@ def tile_list_yard_restack_scores_kernel(
         wg1_sb = held("wg1_sb", [P, S], F32)
         wg2_sb = held("wg2_sb", [P, PN], F32)
         pages = [held("page%d" % m, [P, T2], F32) for m in range(4)]
-        h1 = [held("h1_%d" % b, [P, 4, S], F32) for b in range(2)]
+        h1 = [[held("h1_%d_%d" % (b, t), [P, S], F32) for t in range(4)] for b in range(2)]
+        h2 = [raw_tile("h2_%d" % b, 6 + b) for b in range(2)]
 
         with tc.tile_pool(name="tables", bufs=1) as tables:
             tab_sb = [tables.tile([P, T], I32, name="tab_sb%d" % a) for a in range(2)]
+            tab2_sb = tables.tile([P, T], I32, name="tab2_sb")
             tab_bytes = tables.tile([P, T], U8, name="tab_bytes")
+            tab2_bytes = tables.tile([P, T], U8, name="tab2_bytes")
             w2_sb = tables.tile([P, 2 * H], U8, name="w2_sb")
+            w2_bytes = tables.tile([P, H], U8, name="w2_bytes")
 
-            nc.vector.memset(tab_bytes[:].bitcast(I32), 0)
-            nc.vector.memset(w3_plane[:].rearrange("p a n -> p (a n)").bitcast(I32), 0)
             nc.vector.memset(tab2_bytes[:].bitcast(I32), 0)
             nc.vector.memset(w2_bytes[:].bitcast(I32), 0)
+            nc.vector.memset(tab_bytes[:].bitcast(I32), 0)
+            nc.vector.memset(w3_plane[:].rearrange("p a n -> p (a n)").bitcast(I32), 0)
 
             nc.sync.dma_start(w2_sb[:].bitcast(I32), w2_words[0].bitcast(I32))
-            offs_sb = load_list("offs_sb", offs)
+            offs2_sb = load_list("offs2_sb", offs2)
+            nc.sync.dma_start(tab2_sb[:], table_words(tab2_words, 0))
+            load_scale_rows(tab2_bytes, 0, 4, lambda r: tab2_scales[0, r, :])
             nc.sync.dma_start(tab_sb[0][:], table_words(tab_words, 0))
+            load_scale_rows(w2_bytes, 0, 4, lambda r: w2_scales[0, r, :])
+            offs_sb = load_list("offs_sb", offs)
+            w1_raw = {(0, 0): load_w1(0, 0)}
             load_scale_rows(tab_bytes, 4, 8, lambda r: tab_scales[:, r, :])
             nc.sync.dma_start(tab_sb[1][:], table_words(tab_words, 1))
-            w1_raw = {}
-            for b in range(2):
-                for a in range(2):
-                    w1_raw[a, b] = raw_tile("w1_raw%d%d" % (a, b))
-                    piece = w1[PASS * a : PASS * (a + 1), PASS * b : PASS * (b + 1)]
-                    nc.sync.dma_start(w1_raw[a, b][:], piece.rearrange("(p j) c -> p j c", j=4))
+            w1_raw[1, 0] = load_w1(1, 0)
             nc.sync.dma_start(gain_sb[:], gain.rearrange("(b p t) -> p b t", b=2, t=4))
             pos_sb = load_list("pos_sb", pos1)
+            for a in range(2):
+                w1_raw[a, 1] = load_w1(a, 1)
             nc.sync.dma_start(w3_sb[:].bitcast(I32), w3_words.rearrange("a p c -> p a c").bitcast(I32))
             nc.sync.dma_start(wg1_sb[:], wg1)
             load_page(0)
             load_scale_rows(w3_plane, 0, 4, lambda r: w3_scales[:, r, :].rearrange("a r n -> r a n"))
             offs3_sb = load_list("offs3_sb", offs3)
             load_page(1)
-            load_scale_rows(w2_bytes, 0, 4, lambda r: w2_scales[0, r, :])
-            offs2_sb = load_list("offs2_sb", offs2)
-            nc.sync.dma_start(tab2_sb[:], table_words(tab2_words, 0))
-            load_scale_rows(tab2_bytes, 0, 4, lambda r: tab2_scales[0, r, :])
-            w4_raw = [raw_tile("w4_raw%d" % b) for b in range(2)]
-            nc.sync.dma_start(w4_raw[0][:], w4[0:PASS, :].rearrange("(p j) n -> p j n", j=4))
-            nc.sync.dma_start(w4_raw[1][:], w4[PASS:H, :].rearrange("(p j) n -> p j n", j=4))
+            w4_raw = [load_rows("w4_raw%d" % b, b, w4[PASS * b : PASS * (b + 1), :]) for b in range(2)]
             load_page(2)
             load_page(3)
             offs4_sb = load_list("offs4_sb", offs4)
             nc.sync.dma_start(wg2_sb[:], wg2)
 
-            for b in range(2):
-                cols = slice(2 * PASS * b, 2 * PASS * (b + 1))
-                nc.vector.tensor_copy(w2_dealt[:, cols].rearrange("p (t q e) -> p q t e", t=4, e=2),
-                                      w2_sb[:, cols].rearrange("p (q t e) -> p q t e", t=4, e=2))
+            nc.vector.tensor_copy(w2_dealt[:].rearrange("p (b t q e) -> p b q t e", b=2, t=4, e=2),
+                                  w2_sb[:].rearrange("p (b q t e) -> p b q t e", b=2, t=4, e=2))
+            nc.vector.tensor_copy(v2_words[:], tab2_sb[:].bitcast(U32).indirect(offs2_sb[:]))
+            nc.vector.tensor_copy(v2_plane[:], tab2_bytes[:].indirect(offs2_sb[:]))
+            nc.vector.tensor_copy(w2_plane[:].rearrange("p (b t q) -> p b t q", b=2, t=4),
+                                  w2_bytes[:].rearrange("p (b q t) -> p b t q", b=2, t=4))
             nc.vector.tensor_copy(v_words[0][:], tab_sb[0][:].bitcast(U32).indirect(offs_sb[:]))
             nc.vector.tensor_copy(v_plane[:], tab_bytes[:].indirect(offs_sb[:]))
             nc.vector.tensor_copy(v_words[1][:], tab_sb[1][:].bitcast(U32).indirect(offs_sb[:]))
 
         late = ctx.enter_context(tc.tile_pool(name="late", bufs=1))
 
-        w1_q = {}
+        w1_q = [operand_tiles("w1_%d" % b) for b in range(2)]
         for b in range(2):
+            rounded = rounded_tile("w1_rounded%d" % b, b)
             for a in range(2):
-                rounded = rounded_tile("w1_rounded%d%d" % (a, b), PASS)
                 copy = nc.scalar.copy if (a, b) == (0, 0) else nc.vector.tensor_copy
-                copy(rounded[:].rearrange("p (t m j) -> p m j t", t=4, j=4),
+                copy(half(rounded, a).rearrange("p (t m j) -> p m j t", t=4, j=4),
                      w1_raw[a, b][:].rearrange("p j (m t) -> p m j t", t=4))
-                w1_q[a, b] = quantize("w1_%d%d" % (a, b), rounded, PASS)
+            quantize(w1_q[b], 0, rounded[:])
 
-        def first_stage(acc, b, t, cols):
-            for a in range(2):
-                codes, plane = w1_q[a, b]
+        for b in range(2):
+            for t in range(4):
+                col = PASS * b + P * t
+                acc = bank("h2_acc%d%d" % (b, t))
                 nc.tensor.matmul_mx(
-                    out=acc, lhsT=codes[:, P * t : P * (t + 1)].bitcast(FP8X4),
-                    lhsT_scale=plane[:, P * t : P * (t + 1)], rhs=v_words[a][:, cols].bitcast(FP8X4),
-                    rhs_scale=v_plane[4 * a + 4 :, cols], start=(a == 0), stop=(a == 1))
+                    out=acc[:], lhsT=w2_dealt[:, 2 * col : 2 * (col + P)].bitcast(FP4X4),
+                    lhsT_scale=w2_plane[:, col : col + P], rhs=v2_words[:].bitcast(FP8X4),
+                    rhs_scale=v2_plane[:], start=True, stop=True)
+                nc.scalar.copy(h2[b][:, t, :], acc[:])
 
-        def pair_sums(b, u, cols):
-            acc = bank("h1_pair%d%d_%d" % (b, u, cols.start), "first")
-            for e in range(2):
-                first_stage(acc[:, HEAD * e : HEAD * (e + 1)], b, 2 * u + e, cols)
-            return acc
+        halves = [slice(0, W), slice(W, S)]
 
-        def pair_keep(b, u, cols, acc):
-            nc.scalar.copy(h1[b][:, 2 * u : 2 * u + 2, cols], acc[:].rearrange("p (e n) -> p e n", e=2))
+        def box_features(b, t, c):
+            acc = h1_accs[b, t, c]
+            codes, plane = w1_q[b]
+            for a in range(2):
+                cols = slice(W * a + P * t, W * a + P * (t + 1))
+                nc.tensor.matmul_mx(
+                    out=acc[:], lhsT=codes[:, cols].bitcast(FP8X4), lhsT_scale=plane[:, cols],
+                    rhs=v_words[a][:, halves[c]].bitcast(FP8X4), rhs_scale=v_plane[4 * a + 4 :, halves[c]],
+                    start=(a == 0), stop=(a == 1))
 
         def w3_operand(a, m):
             return w3_sb[:, a, 2 * P * m : 2 * P * (m + 1)].bitcast(FP4X4), w3_plane[:, a, P * m : P * (m + 1)]
 
         def w4_operand(a, m):
-            codes, plane = w4_q[a]
-            return codes[:, P * m : P * (m + 1)].bitcast(FP8X4), plane[:, P * m : P * (m + 1)]
+            cols = slice(W * a + P * m, W * a + P * (m + 1))
+            return w4_q[0][:, cols].bitcast(FP8X4), w4_q[1][:, cols]
 
-        def second_stage(acc, weights, m, z, cols):
+        def scores(name, m, weights, z, places, factors, score):
+            acc = bank("%s_acc%d" % (name, m))
             for a in range(2):
                 lhs, lhs_scale = weights(a, m)
-                nc.tensor.matmul_mx(out=acc, lhsT=lhs, lhsT_scale=lhs_scale, rhs=z[a][0][:, cols].bitcast(FP8X4),
-                                    rhs_scale=z[a][1][:, cols], start=(a == 0), stop=(a == 1))
-
-        def score_tile(name, width):
-            return late.tile([P, width], F32, name=name, tag="score", bufs=4)
-
-        def put(m, places, score, factors):
+                nc.tensor.matmul_mx(out=acc[:], lhsT=lhs, lhsT_scale=lhs_scale,
+                                    rhs=z[0][:, W * a : W * (a + 1)].bitcast(FP8X4),
+                                    rhs_scale=z[1][:, W * a : W * (a + 1)], start=(a == 0), stop=(a == 1))
+            nc.scalar.copy(score, acc[:])
             nc.vector.tensor_tensor(pages[m][:].indirect(places), score, factors, MULT)
 
-        head_cols = slice(0, HEAD)
-        z1_head = []
-        for b in range(2):
-            accs = [pair_sums(b, u, head_cols) for u in range(2)]
-            th = late.tile([P, 2, HEAD, 2], F32, name="tanh_head%d" % b, tag="tanh_head", bufs=2)
-            for u in range(2):
-                nc.scalar.activation(th[:, u, :, :], accs[u][:].rearrange("p (e n) -> p n e", e=2), TANH)
-            rounded = rounded_tile("z1_head_rounded%d" % b, HEAD)
-            factor = gain_sb[:, b, :].rearrange("p (u e) -> p u e", u=2).unsqueeze(1).broadcast_to([P, HEAD, 2, 2])
-            nc.vector.tensor_tensor(rounded[:].rearrange("p (n u e) -> p n u e", u=2, e=2),
-                                    th[:].rearrange("p u n e -> p n u e"), factor, MULT)
-            z1_head.append(quantize("z1_head%d" % b, rounded, HEAD))
-            for u in range(2):
-                pair_keep(b, u, head_cols, accs[u])
+        def score_tile(name):
+            return late.tile([P, W], F32, name=name, tag="score", bufs=4)
 
-        def head_scores(u, score):
-            acc = bank("y1_head_acc%d" % u, "second")
-            for e in range(2):
-                second_stage(acc[:, HEAD * e : HEAD * (e + 1)], w3_operand, 2 * u + e, z1_head, head_cols)
-            nc.scalar.copy(score[:], acc[:])
-            for e in range(2):
-                put(2 * u + e, offs3_sb[:, : HEAD // 16], score[:, HEAD * e : HEAD * (e + 1)], wg1_sb[:, head_cols])
-
-        head_scores(0, score_tile("y1_head0", BANK))
-
-        leads = []
-        for b in range(2):
-            leads.append(raw_tile("lead%d" % b))
-            for u in range(2):
-                cols = slice(HEAD, 2 * HEAD)
-                pair_keep(b, u, cols, pair_sums(b, u, cols))
-                for t in (2 * u, 2 * u + 1):
-                    acc = bank("h1_wide%d%d" % (b, t), "first")
-                    first_stage(acc[:], b, t, slice(2 * HEAD, S))
-                    nc.scalar.copy(h1[b][:, t, 2 * HEAD :], acc[:])
-                    nc.vector.tensor_copy(leads[b][:, t, :], h1[b][:, t, :].indirect(pos_sb[:]))
-
-        nc.vector.tensor_copy(v2_words[:], tab2_sb[:].bitcast(U32).indirect(offs2_sb[:]))
-        nc.vector.tensor_copy(v2_plane[:], tab2_bytes[:].indirect(offs2_sb[:]))
-        nc.vector.tensor_copy(w2_plane[:].rearrange("p (b t q) -> p b t q", b=2, t=4),
-                              w2_bytes[:].rearrange("p (b q t) -> p b t q", b=2, t=4))
-
-        z2 = []
-        for b in range(2):
-            rounded = rounded_tile("z2_rounded%d" % b, PN, "z2_rounded%d" % b, 1)
-            for c in range(PN // P):
-                cols = slice(P * c, P * (c + 1))
-                acc = bank("h2_acc%d%d" % (b, c), "first")
-                for t in range(4):
-                    col = PASS * b + P * t
-                    nc.tensor.matmul_mx(
-                        out=acc[:, P * t : P * (t + 1)], lhsT=w2_dealt[:, 2 * col : 2 * (col + P)].bitcast(FP4X4),
-                        lhsT_scale=w2_plane[:, col : col + P], rhs=v2_words[:, cols].bitcast(FP8X4),
-                        rhs_scale=v2_plane[:, cols], start=True, stop=True)
-                nc.vector.tensor_tensor(
-                    rounded[:, 4 * P * c : 4 * P * (c + 1)].rearrange("p (n i t) -> p n t i", i=2, t=4),
-                    acc[:].rearrange("p (t n i) -> p n t i", t=4, i=2),
-                    leads[b][:, :, cols].rearrange("p t (n i) -> p n t i", i=2), MULT)
-            z2.append(quantize("z2_%d" % b, rounded, PN))
-
-        def planes_tile(b):
-            return late.tile([P, 4, REST], BF16, name="z1_planes%d" % b, tag="z1_planes", bufs=1)
-
-        def rest_plane(planes, b, t):
-            th = late.tile([P, REST], F32, name="tanh_rest%d%d" % (b, t), tag="tanh_rest", bufs=3)
-            nc.scalar.activation(th[:], h1[b][:, t, HEAD:], TANH)
-            nc.scalar.activation(planes[:, t, :], th[:], COPY, scale=gain_sb[:, b, t : t + 1])
+        def box_scores(c, m, z):
+            places = offs3_sb[:, halves[c].start // 16 : halves[c].stop // 16]
+            scores("y1_%d" % c, m, w3_operand, z, places, wg1_sb[:, halves[c]], score_tile("y1_%d%d" % (c, m))[:])
 
         def call_scores(m, score):
-            acc = bank("y2_acc%d" % m, "first")
-            second_stage(acc[:], w4_operand, m, z2, slice(0, PN))
-            nc.scalar.copy(score[:], acc[:])
-            put(m, offs4_sb[:], score[:], wg2_sb[:])
+            scores("y2", m, w4_operand, z2, offs4_sb[:], wg2_sb[:], score)
 
-        planes = planes_tile(0)
-        for t in range(4):
-            rest_plane(planes, 0, t)
-        w4_q = [weave_quantize("w4_%d" % b, w4_raw[b], N) for b in range(2)]
-        z1_rest = [weave_quantize("z1_rest0", planes, REST, "rest_rounded", 1)]
-        head_scores(1, ring.tile([P, BANK], F32, name="y1_head1", tag="z2_rounded1", bufs=1, align_bytes=64))
-        planes = planes_tile(1)
-        for t in range(4):
-            rest_plane(planes, 1, t)
-            if t > 0:
-                call_scores(t - 1, score_tile("y2_%d" % (t - 1), PN))
-        z1_rest.append(weave_quantize("z1_rest1", planes, REST, "rest_rounded", 1))
-        call_scores(3, late.tile([P, PN], F32, name="y2_last", tag="z1_planes", bufs=1))
+        order = [(0, t, c) for t in range(4) for c in range(2)] + [(1, t, c) for c in range(2) for t in range(4)]
+        h1_accs = {key: bank("h1_acc%d%d%d" % key) for key in order}
 
+        z1_first = operand_tiles("z1_first")
+        for b, tag in enumerate(("rounded1", "raw6")):
+            rounded = ring.tile([P, 4 * W], BF16, name="z1_first_rounded%d" % b, tag=tag, align_bytes=64)
+            for c in range(2):
+                for t in range(4):
+                    box_features(b, t, c)
+            th = raw_tile("tanh_first%d" % b, 4 + b)
+            for t in range(4):
+                nc.scalar.activation(th[:, t, :], h1_accs[b, t, 0][:], TANH)
+            factor = gain_sb[:, b, :].unsqueeze(1).unsqueeze(3).broadcast_to([P, W // 2, 4, 2])
+            nc.vector.tensor_tensor(rounded[:].rearrange("p (n i t) -> p n t i", i=2, t=4),
+                                    th[:].rearrange("p t (n i) -> p n t i", i=2), factor, MULT)
+            quantize(z1_first, W * b, rounded[:])
+
+        prods = []
+        for b in range(2):
+            prods.append(raw_tile("z2_raw%d" % b, (4, 6)[b]))
+            for t in range(4):
+                for c in range(2):
+                    nc.scalar.copy(h1[b][t][:, halves[c]], h1_accs[b, t, c][:])
+                nc.vector.tensor_tensor(prods[b][:, t, :], h1[b][t][:].indirect(pos_sb[:]), h2[b][:, t, :], MULT)
+        for m in range(2):
+            box_scores(0, m, z1_first)
+
+        w4_q, z2, z1_second = operand_tiles("w4"), operand_tiles("z2"), operand_tiles("z1_second")
+        rounded = rounded_tile("w4_rounded", 0)
+        for b in range(2):
+            weave(half(rounded, b), w4_raw[b])
+        quantize(w4_q, 0, rounded[:])
+        rounded = rounded_tile("z2_rounded", 1)
+        weave(half(rounded, 0), prods[0])
+        box_scores(0, 2, z1_first)
+        weave(half(rounded, 1), prods[1])
+        quantize(z2, 0, rounded[:])
+        box_scores(0, 3, z1_first)
+
+        rounded = rounded_tile("z1_second_rounded", 0)
+        for b in range(2):
+            th = raw_tile("tanh_second%d" % b, 5)
+            planes = late.tile([P, 4, W], BF16, name="z1_planes%d" % b, tag="planes%d" % b)
+            for t in range(4):
+                nc.scalar.activation(th[:, t, :], h1[b][t][:, halves[1]], TANH)
+                nc.scalar.activation(planes[:, t, :], th[:, t, :], COPY, scale=gain_sb[:, b, t : t + 1])
+            weave(half(rounded, b), planes)
+            if b == 0:
+                early = late.tile([P, 3, W], F32, name="y2_early", tag="planes0")
+                for m in range(3):
+                    call_scores(m, early[:, m, :])
+        quantize(z1_second, 0, rounded[:])
+        last = late.tile([P, W], F32, name="y2_3", tag="planes1")
+        call_scores(3, last[:])
         for m in range(4):
-            score = score_tile("y1_rest%d" % m, REST)
-            for lo in range(0, REST, BANK):
-                cols = slice(lo, min(lo + BANK, REST))
-                acc = bank("y1_rest_acc%d_%d" % (m, lo), "first")
-                second_stage(acc[:, : cols.stop - lo], w3_operand, m, z1_rest, cols)
-                nc.scalar.copy(score[:, cols], acc[:, : cols.stop - lo])
-            put(m, offs3_sb[:, HEAD // 16 :], score[:], wg1_sb[:, HEAD:])
+            box_scores(1, m, z1_second)
             nc.sync.dma_start(out[P * m : P * (m + 1), :], pages[m][:])

from contextlib import ExitStack

import concourse.mybir as mybir

K, K2, H, N, T, S, PN, T2 = 1024, 512, 1024, 512, 2048, 1024, 512, 2048
FLOPS = 2 * (K * H * S + K2 * H * PN + H * N * S + H * N * PN)

F32 = mybir.dt.float32
BF16 = mybir.dt.bfloat16
I32 = mybir.dt.int32
U32 = mybir.dt.uint32
U16 = mybir.dt.uint16
U8 = mybir.dt.uint8
FP8X4 = mybir.dt.float8_e4m3fn_x4
FP4X4 = mybir.dt.float4_e2m1fn_x4
MULT = mybir.AluOpType.mult
TANH = mybir.ActivationFunctionType.Tanh
COPY = mybir.ActivationFunctionType.Copy

P = 128
PASS = 512
W = 512


def tile_list_yard_restack_scores_kernel(
    tc, tab_words, tab_scales, tab2_words, tab2_scales, w1, w2_words, w2_scales, gain,
    w3_words, w3_scales, w4, page1, wg1, wg2, offs, offs2, pos1, offs3, offs4, out,
):
    nc = tc.nc
    with ExitStack() as ctx:
        lists = ctx.enter_context(tc.tile_pool(name="lists", bufs=1))
        keep = ctx.enter_context(tc.tile_pool(name="keep", bufs=1))
        ring = ctx.enter_context(tc.tile_pool(name="ring", bufs=1))
        psum = ctx.enter_context(tc.psum_pool(name="psum", bufs=1))

        def held(name, shape, dtype):
            return keep.tile(shape, dtype, name=name, align_bytes=64)

        def load_list(name, src):
            tile = lists.tile(list(src.shape), U16, name=name)
            nc.sync.dma_start(tile[:], src)
            return tile

        def raw_tile(name, room):
            return ring.tile([P, 4, W], F32, name=name, tag="raw%d" % room, align_bytes=64)

        def rounded_tile(name, room):
            return ring.tile([P, 2 * 4 * W], BF16, name=name, tag="rounded%d" % room, align_bytes=64)

        def half(rounded, a):
            return rounded[:, 4 * W * a : 4 * W * (a + 1)]

        banks = []

        def bank(name):
            banks.append(psum.tile([P, W], F32, name=name, tag="bank%d" % (len(banks) % 8), bufs=1))
            return banks[-1]

        def operand_tiles(name):
            return held(name + "_codes", [P, 2 * W], U32), held(name + "_plane", [P, 2 * W], U8)

        def quantize(operand, first, rounded):
            cols = slice(first, first + rounded.shape[1] // 4)
            nc.vector.quantize_mx(out=operand[0][:, cols].bitcast(FP8X4), scales=operand[1][:, cols], in_=rounded)

        def weave(dst, src):
            nc.scalar.copy(dst.rearrange("p (c i j) -> p c j i", i=4, j=4),
                           src[:].rearrange("p j (c i) -> p c j i", i=4))

        def table_words(words, a):
            return words[a].rearrange("p t i -> p (t i)").bitcast(I32)

        def load_scale_rows(plane, first, rows, scales):
            for q in range(4):
                lo = 32 * q + first
                nc.sync.dma_start(plane[lo : lo + rows].bitcast(I32), scales(slice(4 * q, 4 * q + 4)).bitcast(I32))

        def load_rows(name, room, rows):
            raw = raw_tile(name, room)
            nc.sync.dma_start(raw[:], rows.rearrange("(p j) c -> p j c", j=4))
            return raw

        def load_w1(a, b):
            return load_rows("w1_raw%d%d" % (a, b), 2 * b + a, w1[PASS * a : PASS * (a + 1), W * b : W * (b + 1)])

        def load_page(m):
            nc.sync.dma_start(pages[m][:], page1[P * m : P * (m + 1), :])

        v_words = [held("v_words%d" % a, [P, S], U32) for a in range(2)]
        v_plane = held("v_plane", [P, S], U8)
        v2_words = held("v2_words", [P, PN], U32)
        v2_plane = held("v2_plane", [P, PN], U8)
        w2_dealt = held("w2_dealt", [P, 2 * H], U8)
        w2_plane = held("w2_plane", [P, H], U8)
        w3_sb = held("w3_sb", [P, 2, 2 * N], U8)
        w3_plane = held("w3_plane", [P, 2, N], U8)
        gain_sb = held("gain_sb", [P, 2, 4], F32)
        wg1_sb = held("wg1_sb", [P, S], F32)
        wg2_sb = held("wg2_sb", [P, PN], F32)
        pages = [held("page%d" % m, [P, T2], F32) for m in range(4)]
        h1 = [[held("h1_%d_%d" % (b, t), [P, S], F32) for t in range(4)] for b in range(2)]
        h2 = [raw_tile("h2_%d" % b, 6 + b) for b in range(2)]

        with tc.tile_pool(name="tables", bufs=1) as tables:
            tab_sb = [tables.tile([P, T], I32, name="tab_sb%d" % a) for a in range(2)]
            tab2_sb = tables.tile([P, T], I32, name="tab2_sb")
            tab_bytes = tables.tile([P, T], U8, name="tab_bytes")
            tab2_bytes = tables.tile([P, T], U8, name="tab2_bytes")
            w2_sb = tables.tile([P, 2 * H], U8, name="w2_sb")
            w2_bytes = tables.tile([P, H], U8, name="w2_bytes")

            nc.vector.memset(tab2_bytes[:].bitcast(I32), 0)
            nc.vector.memset(w2_bytes[:].bitcast(I32), 0)
            nc.vector.memset(tab_bytes[:].bitcast(I32), 0)
            nc.vector.memset(w3_plane[:].rearrange("p a n -> p (a n)").bitcast(I32), 0)

            nc.sync.dma_start(w2_sb[:].bitcast(I32), w2_words[0].bitcast(I32))
            offs2_sb = load_list("offs2_sb", offs2)
            nc.sync.dma_start(tab2_sb[:], table_words(tab2_words, 0))
            load_scale_rows(tab2_bytes, 0, 4, lambda r: tab2_scales[0, r, :])
            nc.sync.dma_start(tab_sb[0][:], table_words(tab_words, 0))
            load_scale_rows(w2_bytes, 0, 4, lambda r: w2_scales[0, r, :])
            offs_sb = load_list("offs_sb", offs)
            w1_raw = {(0, 0): load_w1(0, 0)}
            load_scale_rows(tab_bytes, 4, 8, lambda r: tab_scales[:, r, :])
            nc.sync.dma_start(tab_sb[1][:], table_words(tab_words, 1))
            w1_raw[1, 0] = load_w1(1, 0)
            nc.sync.dma_start(gain_sb[:], gain.rearrange("(b p t) -> p b t", b=2, t=4))
            pos_sb = load_list("pos_sb", pos1)
            for a in range(2):
                w1_raw[a, 1] = load_w1(a, 1)
            nc.sync.dma_start(w3_sb[:].bitcast(I32), w3_words.rearrange("a p c -> p a c").bitcast(I32))
            nc.sync.dma_start(wg1_sb[:], wg1)
            load_page(0)
            load_scale_rows(w3_plane, 0, 4, lambda r: w3_scales[:, r, :].rearrange("a r n -> r a n"))
            offs3_sb = load_list("offs3_sb", offs3)
            load_page(1)
            w4_raw = [load_rows("w4_raw%d" % b, b, w4[PASS * b : PASS * (b + 1), :]) for b in range(2)]
            load_page(2)
            load_page(3)
            offs4_sb = load_list("offs4_sb", offs4)
            nc.sync.dma_start(wg2_sb[:], wg2)

            nc.vector.tensor_copy(w2_dealt[:].rearrange("p (b t q e) -> p b q t e", b=2, t=4, e=2),
                                  w2_sb[:].rearrange("p (b q t e) -> p b q t e", b=2, t=4, e=2))
            nc.vector.tensor_copy(v2_words[:], tab2_sb[:].bitcast(U32).indirect(offs2_sb[:]))
            nc.vector.tensor_copy(v2_plane[:], tab2_bytes[:].indirect(offs2_sb[:]))
            nc.vector.tensor_copy(w2_plane[:].rearrange("p (b t q) -> p b t q", b=2, t=4),
                                  w2_bytes[:].rearrange("p (b q t) -> p b t q", b=2, t=4))
            nc.vector.tensor_copy(v_words[0][:], tab_sb[0][:].bitcast(U32).indirect(offs_sb[:]))
            nc.vector.tensor_copy(v_plane[:], tab_bytes[:].indirect(offs_sb[:]))
            nc.vector.tensor_copy(v_words[1][:], tab_sb[1][:].bitcast(U32).indirect(offs_sb[:]))

        late = ctx.enter_context(tc.tile_pool(name="late", bufs=1))

        w1_q = [operand_tiles("w1_%d" % b) for b in range(2)]
        for b in range(2):
            rounded = rounded_tile("w1_rounded%d" % b, b)
            for a in range(2):
                copy = nc.scalar.copy if (a, b) == (0, 0) else nc.vector.tensor_copy
                copy(half(rounded, a).rearrange("p (t m j) -> p m j t", t=4, j=4),
                     w1_raw[a, b][:].rearrange("p j (m t) -> p m j t", t=4))
            quantize(w1_q[b], 0, rounded[:])

        for b in range(2):
            for t in range(4):
                col = PASS * b + P * t
                acc = bank("h2_acc%d%d" % (b, t))
                nc.tensor.matmul_mx(
                    out=acc[:], lhsT=w2_dealt[:, 2 * col : 2 * (col + P)].bitcast(FP4X4),
                    lhsT_scale=w2_plane[:, col : col + P], rhs=v2_words[:].bitcast(FP8X4),
                    rhs_scale=v2_plane[:], start=True, stop=True)
                nc.scalar.copy(h2[b][:, t, :], acc[:])

        halves = [slice(0, W), slice(W, S)]

        def box_features(b, t, c):
            acc = h1_accs[b, t, c]
            codes, plane = w1_q[b]
            for a in range(2):
                cols = slice(W * a + P * t, W * a + P * (t + 1))
                nc.tensor.matmul_mx(
                    out=acc[:], lhsT=codes[:, cols].bitcast(FP8X4), lhsT_scale=plane[:, cols],
                    rhs=v_words[a][:, halves[c]].bitcast(FP8X4), rhs_scale=v_plane[4 * a + 4 :, halves[c]],
                    start=(a == 0), stop=(a == 1))

        def w3_operand(a, m):
            return w3_sb[:, a, 2 * P * m : 2 * P * (m + 1)].bitcast(FP4X4), w3_plane[:, a, P * m : P * (m + 1)]

        def w4_operand(a, m):
            cols = slice(W * a + P * m, W * a + P * (m + 1))
            return w4_q[0][:, cols].bitcast(FP8X4), w4_q[1][:, cols]

        def scores(name, m, weights, z, places, factors, score):
            acc = bank("%s_acc%d" % (name, m))
            for a in range(2):
                lhs, lhs_scale = weights(a, m)
                nc.tensor.matmul_mx(out=acc[:], lhsT=lhs, lhsT_scale=lhs_scale,
                                    rhs=z[0][:, W * a : W * (a + 1)].bitcast(FP8X4),
                                    rhs_scale=z[1][:, W * a : W * (a + 1)], start=(a == 0), stop=(a == 1))
            nc.scalar.copy(score, acc[:])
            nc.vector.tensor_tensor(pages[m][:].indirect(places), score, factors, MULT)

        def score_tile(name):
            return late.tile([P, W], F32, name=name, tag="score", bufs=4)

        def box_scores(c, m, z):
            places = offs3_sb[:, halves[c].start // 16 : halves[c].stop // 16]
            scores("y1_%d" % c, m, w3_operand, z, places, wg1_sb[:, halves[c]], score_tile("y1_%d%d" % (c, m))[:])

        def call_scores(m, score):
            scores("y2", m, w4_operand, z2, offs4_sb[:], wg2_sb[:], score)

        order = [(0, t, c) for t in range(4) for c in range(2)] + [(1, t, c) for c in range(2) for t in range(4)]
        h1_accs = {key: bank("h1_acc%d%d%d" % key) for key in order}

        z1_first = operand_tiles("z1_first")
        for b, tag in enumerate(("rounded1", "raw6")):
            rounded = ring.tile([P, 4 * W], BF16, name="z1_first_rounded%d" % b, tag=tag, align_bytes=64)
            for c in range(2):
                for t in range(4):
                    box_features(b, t, c)
            th = raw_tile("tanh_first%d" % b, 4 + b)
            for t in range(4):
                nc.scalar.activation(th[:, t, :], h1_accs[b, t, 0][:], TANH)
            factor = gain_sb[:, b, :].unsqueeze(1).unsqueeze(3).broadcast_to([P, W // 2, 4, 2])
            nc.vector.tensor_tensor(rounded[:].rearrange("p (n i t) -> p n t i", i=2, t=4),
                                    th[:].rearrange("p t (n i) -> p n t i", i=2), factor, MULT)
            quantize(z1_first, W * b, rounded[:])

        prods = []
        for b in range(2):
            prods.append(raw_tile("z2_raw%d" % b, (4, 6)[b]))
            for t in range(4):
                for c in range(2):
                    nc.scalar.copy(h1[b][t][:, halves[c]], h1_accs[b, t, c][:])
                nc.vector.tensor_tensor(prods[b][:, t, :], h1[b][t][:].indirect(pos_sb[:]), h2[b][:, t, :], MULT)
        for m in range(2):
            box_scores(0, m, z1_first)

        w4_q, z2, z1_second = operand_tiles("w4"), operand_tiles("z2"), operand_tiles("z1_second")
        rounded = rounded_tile("w4_rounded", 0)
        for b in range(2):
            weave(half(rounded, b), w4_raw[b])
        quantize(w4_q, 0, rounded[:])
        rounded = rounded_tile("z2_rounded", 1)
        weave(half(rounded, 0), prods[0])
        box_scores(0, 2, z1_first)
        weave(half(rounded, 1), prods[1])
        quantize(z2, 0, rounded[:])
        box_scores(0, 3, z1_first)

        rounded = rounded_tile("z1_second_rounded", 0)
        for b in range(2):
            th = raw_tile("tanh_second%d" % b, 5)
            planes = late.tile([P, 4, W], BF16, name="z1_planes%d" % b, tag="planes%d" % b)
            for t in range(4):
                nc.scalar.activation(th[:, t, :], h1[b][t][:, halves[1]], TANH)
                nc.scalar.activation(planes[:, t, :], th[:, t, :], COPY, scale=gain_sb[:, b, t : t + 1])
            weave(half(rounded, b), planes)
            if b == 0:
                early = late.tile([P, 3, W], F32, name="y2_early", tag="planes0")
                for m in range(3):
                    call_scores(m, early[:, m, :])
        quantize(z1_second, 0, rounded[:])
        last = late.tile([P, W], F32, name="y2_3", tag="planes1")
        call_scores(3, last[:])
        for m in range(4):
            box_scores(1, m, z1_second)
            nc.sync.dma_start(out[P * m : P * (m + 1), :], pages[m][:])
